import numpy as np
import ml_dtypes


def mxq(x, axis, fmt="e4m3"):
    dtype, down = {"e4m3": (ml_dtypes.float8_e4m3fn, 7), "e5m2": (ml_dtypes.float8_e5m2, 14)}[fmt]
    v = np.moveaxis(np.asarray(x, np.float32).astype(ml_dtypes.bfloat16).astype(np.float64), axis, -1)
    blocks = v.reshape(v.shape[:-1] + (-1, 32))
    amax = np.abs(blocks).max(-1, keepdims=True)
    byte = np.maximum(np.where(amax > 0, np.frexp(amax)[1] - 1 + 127, 0) - down, 1)
    scale = np.exp2(byte - 127.0)
    codes = (blocks / scale).astype(np.float32).astype(dtype).astype(np.float64)
    return np.moveaxis((codes * scale).reshape(v.shape), -1, axis)


WIDE = False


def mx_kscale(k):
    if not WIDE:
        return np.ones(k)
    levels = np.array([10, -10, 5, -5, 0])
    if k % 512:
        return np.exp2(np.random.permutation(np.resize(levels, k // 32))).repeat(32)
    a = np.empty((k // 512, 16))
    for p in range(k // 512):
        a[p, :8] = np.random.permutation(np.resize(levels, 8))
        for g in range(8):
            far = levels[np.abs(levels - a[p, g]) >= 10]
            a[p, g + 8] = far[np.random.randint(len(far))]
    return np.exp2(a.ravel()).repeat(32)


def f64(x):
    return np.asarray(x).astype(np.float64)


def striped(idx):
    return np.tile(np.asarray(idx).reshape(-1, 16).T, (8, 1)).astype(np.uint16)


def unstriped(offs):
    return offs[:16].T.reshape(-1).astype(np.int64)


def bf(x):
    return np.asarray(x, np.float32).astype(ml_dtypes.bfloat16)


def planes(Y):
    r, m = Y.shape
    b = f64(bf(Y)).reshape(r // 32, 32, m)
    amax = np.abs(b).max(1)
    byte = np.clip(np.where(amax > 0, np.frexp(amax)[1] - 1 + 127 - 7, 1), 1, 254)
    codes = (b * np.exp2(127.0 - byte)[:, None, :]).reshape(r, m).astype(np.float32).astype(ml_dtypes.float8_e4m3fn).view(np.uint8)
    words = codes.reshape(r // 512, 128, 4, m).transpose(0, 1, 3, 2)
    return np.ascontiguousarray(words), np.ascontiguousarray(byte.astype(np.uint8).reshape(r // 512, 16, m))


T, I, Q, E, K, F = 2048, 512, 256, 512, 512, 512


def setup_inputs():
    n = np.random.standard_normal
    idx = np.random.permutation(T)[:I]
    fk = mx_kscale(K)
    ff = mx_kscale(F)
    fi = mx_kscale(I)
    ti = np.ones(T)
    ti[idx] = fi
    return {
        "inp": (n((K, Q)) * fk[:, None]).astype(np.float32),
        "w1": (n((K, F)) * 1 / np.sqrt(K) / fk[:, None] * ff).astype(np.float32),
        "w2": (n((F, I)) * 1.2 / np.sqrt(F) / ff[:, None]).astype(np.float32),
        "size": (np.random.uniform(0.5, 2.0, (1, I)) * fi).astype(np.float32),
        "vals": (n((E, T)) / ti).astype(np.float32),
        "res": (n((E, Q)) * 0.25).astype(np.float32),
        "offs": striped(idx),
    }


def reference(inp, w1, w2, size, vals, res, offs):
    idx = unstriped(offs)
    w1q = mxq(f64(w1), 0, "e4m3")
    inpq = mxq(f64(inp), 0, "e4m3")
    z = w1q.T @ inpq
    g = np.maximum(z, 0.0)
    gq = mxq(g, 0, "e4m3")
    w2q = mxq(f64(w2), 0, "e4m3")
    a = gq.T @ w2q
    p = np.exp(a - np.max(a, axis=1, keepdims=True))
    w = p * f64(size) / np.sum(p, axis=1, keepdims=True)
    wt = w.T
    vt = f64(vals)[:, idx].T
    vtq = mxq(vt, 0, "e4m3")
    wtq = mxq(wt, 0, "e4m3")
    o = vtq.T @ wtq
    y = o + f64(res)
    words, scales = planes(y)
    return y, words, scales

@@ -1,0 +1,227 @@
+from contextlib import ExitStack
+
+import concourse.mybir as mybir
+from concourse.masks import make_identity
+
+T, I, Q, E, K, F = 2048, 512, 256, 512, 512, 512
+FLOPS = 2 * Q * (K * F + F * I + I * E)
+
+F32 = mybir.dt.float32
+BF16 = mybir.dt.bfloat16
+I32 = mybir.dt.int32
+U32 = mybir.dt.uint32
+U16 = mybir.dt.uint16
+U8 = mybir.dt.uint8
+FP8X4 = mybir.dt.float8_e4m3fn_x4
+ALU = mybir.AluOpType
+ACT = mybir.ActivationFunctionType
+AX = mybir.AxisListType
+
+P = 128
+PACK = 4
+HALVES = Q // P
+W1_SPLIT = 88
+W2_SPLIT = 352
+Y_SPLIT = 168
+
+
+def tile_attend_synthesizer_pl_kernel(tc, inp, w1, w2, size, vals, res, offs, out_0, out_1, out_2):
+    nc = tc.nc
+
+    with ExitStack() as ctx:
+        sb = ctx.enter_context(tc.tile_pool(name="sb", bufs=1))
+        ps = ctx.enter_context(tc.psum_pool(name="ps", bufs=1))
+
+        def quantize(codes, scales, grouped):
+            nc.vector.quantize_mx(out=codes.bitcast(FP8X4), scales=scales, in_=grouped)
+
+        def matmul(out, lhs_codes, lhs_scales, rhs_codes, rhs_scales):
+            nc.tensor.matmul_mx(
+                out=out,
+                lhsT=lhs_codes.bitcast(FP8X4),
+                lhsT_scale=lhs_scales,
+                rhs=rhs_codes.bitcast(FP8X4),
+                rhs_scale=rhs_scales,
+                start=True,
+                stop=True,
+            )
+
+        def operand(name, width):
+            codes = sb.tile([P, width], U32, name=name + "_codes", align_bytes=64)
+            scales = sb.tile([P, width], U8, name=name + "_scales", align_bytes=64)
+            return codes, scales
+
+        def interleave(on_vector, grouped, raw, c0, c1):
+            dst = grouped[:].rearrange("p (c i t) -> p c t i", i=PACK, t=PACK)[:, c0 // PACK : c1 // PACK]
+            src = raw[:].rearrange("p t (c i) -> p c t i", i=PACK)[:, c0 // PACK : c1 // PACK]
+            if on_vector:
+                nc.vector.tensor_copy(out=dst, in_=src)
+            else:
+                nc.scalar.activation(out=dst, in_=src, func=ACT.Copy)
+
+        size_cols = sb.tile([P, PACK], F32)
+        nc.scalar.dma_start(out=size_cols[:], in_=size.rearrange("o (p t) -> p (o t)", t=PACK))
+        w1_raw = sb.tile([P, PACK, F], F32)
+        nc.sync.dma_start(out=w1_raw[:], in_=w1.rearrange("(p j) f -> p j f", j=PACK))
+        inp_raw = sb.tile([P, PACK, Q], F32)
+        nc.sync.dma_start(out=inp_raw[:], in_=inp.rearrange("(p j) q -> p j q", j=PACK))
+        w2_raw = sb.tile([P, PACK, I], F32)
+        nc.sync.dma_start(out=w2_raw[:], in_=w2.rearrange("(p j) i -> p j i", j=PACK))
+        offsets = sb.tile([P, I // 16], U16)
+        nc.sync.dma_start(offsets[:], offs)
+        vals_rows = vals.rearrange("(p t) c -> p t c", t=PACK)
+        pools = []
+        for t in range(PACK):
+            pool_t = sb.tile([P, T], F32, name="pool%d" % t, tag="pool%d" % t, align_bytes=64)
+            nc.sync.dma_start(out=pool_t[:], in_=vals_rows[:, t, :])
+            pools.append(pool_t)
+        res_sb = sb.tile([P, PACK, Q], F32)
+        nc.sync.dma_start(out=res_sb[:], in_=res.rearrange("(p t) q -> p t q", t=PACK))
+
+        ident = sb.tile([P, P], F32)
+        make_identity(nc, ident[:])
+
+        size_bank = ps.tile([P, PACK, P], F32, tag="bank4")
+        for t in range(PACK):
+            nc.tensor.transpose(size_bank[:, t, :], size_cols[:, t : t + 1].to_broadcast([P, P]), ident[:])
+
+        size_row = sb.tile([P, I], F32)
+        nc.scalar.copy(
+            out=size_row[:].rearrange("q (u g m t) -> q u g m t", u=2, m=PACK, t=PACK),
+            in_=size_bank[:].rearrange("q t (g u m) -> q u g m t", u=2, m=PACK),
+        )
+
+        w1_grp = sb.tile([P, F * PACK], BF16, align_bytes=64)
+        w1_dst = w1_grp[:].rearrange("p (t m j) -> p m j t", t=PACK, j=PACK)
+        w1_src = w1_raw[:].rearrange("p j (m t) -> p m j t", t=PACK)
+        nc.vector.tensor_copy(out=w1_dst[:, :W1_SPLIT], in_=w1_src[:, :W1_SPLIT])
+        nc.scalar.activation(out=w1_dst[:, W1_SPLIT:], in_=w1_src[:, W1_SPLIT:], func=ACT.Copy)
+        w1_codes, w1_scales = operand("w1", F)
+        quantize(w1_codes[:], w1_scales[:], w1_grp[:])
+
+        inp_grp = sb.tile([P, Q * PACK], BF16, align_bytes=64)
+        interleave(True, inp_grp, inp_raw, 0, P)
+        interleave(False, inp_grp, inp_raw, P, Q)
+        inp_ops = [operand("inp%d" % h, P) for h in range(HALVES)]
+        z_banks = [ps.tile([P, PACK, P], F32, name="z%d" % h, tag="bank%d" % h) for h in range(HALVES)]
+        g_grp = [sb.tile([P, P * PACK], BF16, name="g_grp%d" % h, align_bytes=64) for h in range(HALVES)]
+        for h in range(HALVES):
+            quantize(inp_ops[h][0][:], inp_ops[h][1][:], inp_grp[:, h * P * PACK : (h + 1) * P * PACK])
+            for t in range(PACK):
+                m_cols = slice(t * P, (t + 1) * P)
+                matmul(z_banks[h][:, t, :], w1_codes[:, m_cols], w1_scales[:, m_cols], inp_ops[h][0][:], inp_ops[h][1][:])
+
+        def relu(h):
+            nc.scalar.activation(
+                out=g_grp[h][:].rearrange("p (q t) -> p q t", t=PACK),
+                in_=z_banks[h][:].rearrange("p t q -> p q t"),
+                func=ACT.Relu,
+            )
+
+        w2_grp = sb.tile([P, I * PACK], BF16, align_bytes=64, tag="hold0")
+        relu(0)
+        interleave(True, w2_grp, w2_raw, 0, W2_SPLIT)
+        interleave(False, w2_grp, w2_raw, W2_SPLIT, I)
+        relu(1)
+        w2_codes, w2_scales = operand("w2", I)
+        g_ops = [operand("g%d" % h, P) for h in range(HALVES)]
+        quantize(g_ops[0][0][:], g_ops[0][1][:], g_grp[0][:])
+        quantize(w2_codes[:], w2_scales[:], w2_grp[:])
+        quantize(g_ops[1][0][:], g_ops[1][1][:], g_grp[1][:])
+        a_banks = [ps.tile([P, I], F32, name="a%d" % h, tag="bank%d" % (2 + h)) for h in range(HALVES)]
+        for h in range(HALVES):
+            matmul(a_banks[h][:], g_ops[h][0][:], g_ops[h][1][:], w2_codes[:], w2_scales[:])
+
+        def turn(name, rows_bf16, bank_tag):
+            words = rows_bf16[:].bitcast(F32)
+            bank = ps.tile([P, 2, P], F32, name=name + "_bank", tag=bank_tag)
+            for u in range(2):
+                nc.tensor.transpose(bank[:, u, :], words[:, u * P : (u + 1) * P], ident[:])
+            grp = sb.tile([P, P * PACK], BF16, name=name + "_grp", align_bytes=64)
+            nc.scalar.copy(
+                out=grp[:].bitcast(F32).rearrange("p (x u) -> p x u", u=2),
+                in_=bank[:].rearrange("p u x -> p x u"),
+            )
+            return grp
+
+        pick = {}
+
+        def gather(t):
+            picked = sb.tile([P, I], BF16, name="picked%d" % t, align_bytes=64, tag=("hold0", "hold0", "hold2", "hold3")[t])
+            nc.vector.tensor_copy(
+                picked[:].rearrange("p (u g r) -> p g u r", u=2, r=16), pools[t][:].indirect(offsets[:])
+            )
+            pick[t] = picked
+            return turn("vt%d" % t, picked, "bank%d" % (t % 2))
+
+        vt_ops = [operand("vt%d" % t, P) if t == 3 else (None, sb.tile([P, P], U8, name="vt%d_scales" % t, align_bytes=64)) for t in range(PACK)]
+
+        def quantize_vt(t, grp):
+            quantize(vt_ops[t][0][:], vt_ops[t][1][:], grp[:])
+
+        row_sum = sb.tile([P, HALVES], F32)
+        probs = [sb.tile([P, I], F32, name="probs%d" % h, align_bytes=64, tag="hold%d" % (2 + h)) for h in range(HALVES)]
+        vt_grp0 = gather(0)
+        neg_max = sb.tile([P, HALVES], F32, align_bytes=64, tag="pool0")
+        for h in range(HALVES):
+            nc.vector.tensor_reduce(out=neg_max[:, h : h + 1], in_=a_banks[h][:], axis=AX.X, op=ALU.max, negate=True)
+            nc.scalar.activation(
+                out=probs[h][:].rearrange("q (u g r) -> q u g r", u=2, r=16),
+                in_=a_banks[h][:].rearrange("q (g u r) -> q u g r", u=2, r=16), func=ACT.Exp, bias=neg_max[:, h : h + 1], scale=1.0, accum_out=row_sum[:, h : h + 1]
+            )
+        vt_grp1 = gather(1)
+        inv_sum = sb.tile([P, HALVES], F32, align_bytes=64, tag="pool1")
+        nc.vector.reciprocal(out=inv_sum[:], in_=row_sum[:])
+        wt_grp = []
+        for h in range(HALVES):
+            weights = sb.tile([P, I], BF16, name="weights%d" % h, align_bytes=64)
+            nc.vector.scalar_tensor_tensor(
+                out=weights[:],
+                in0=probs[h][:],
+                scalar=inv_sum[:, h : h + 1],
+                in1=size_row[:],
+                op0=ALU.mult,
+                op1=ALU.mult,
+            )
+            wt_grp.append(turn("wt%d" % h, weights, "bank%d" % (5 + h)))
+        vt_grp2 = gather(2)
+        vt_grp3 = gather(3)
+        late_codes = sb.tile([P, Q + 3 * P], U32, align_bytes=64, tag="pool3")
+        wt_codes = late_codes[:, :Q]
+        wt_scales = sb.tile([P, Q], U8, align_bytes=64)
+        for t in range(3):
+            vt_ops[t] = (late_codes[:, Q + t * P : Q + (t + 1) * P], vt_ops[t][1])
+        for h in range(HALVES):
+            q_cols = slice(h * P, (h + 1) * P)
+            quantize(wt_codes[:, q_cols], wt_scales[:, q_cols], wt_grp[h][:])
+        quantize_vt(0, vt_grp0)
+        quantize_vt(1, vt_grp1)
+        quantize_vt(2, vt_grp2)
+        quantize_vt(3, vt_grp3)
+
+        o01 = ps.tile([P, 2, Q], F32, tag="bank2")
+        o2 = ps.tile([P, Q], F32, tag="bank3")
+        o3 = ps.tile([P, Q], F32, tag="bank7")
+        y = sb.tile([P, PACK, Q], F32)
+        out_rows = out_0.rearrange("(p t) q -> p t q", t=PACK)
+        for t, o in ((0, o01[:, 0, :]), (1, o01[:, 1, :]), (2, o2[:])):
+            matmul(o, vt_ops[t][0][:], vt_ops[t][1][:], wt_codes[:], wt_scales[:])
+        nc.vector.tensor_tensor(out=y[:, 0:2, :], in0=o01[:], in1=res_sb[:, 0:2, :], op=ALU.add)
+        nc.vector.tensor_tensor(out=y[:, 2, :], in0=o2[:], in1=res_sb[:, 2, :], op=ALU.add)
+        nc.sync.dma_start(out=out_rows[:, 0:3, :], in_=y[:, 0:3, :])
+        matmul(o3[:], vt_ops[3][0][:], vt_ops[3][1][:], wt_codes[:], wt_scales[:])
+        nc.vector.tensor_tensor(out=y[:, 3, :], in0=o3[:], in1=res_sb[:, 3, :], op=ALU.add)
+        nc.sync.dma_start(out=out_rows[:, 3, :], in_=y[:, 3, :])
+
+        y_grp = sb.tile([P, Q * PACK], BF16, align_bytes=64)
+        interleave(True, y_grp, y, 0, Y_SPLIT)
+        interleave(False, y_grp, y, Y_SPLIT, Q)
+        y_codes, y_scales = operand("y", Q)
+        quantize(y_codes[:], y_scales[:], y_grp[:])
+        nc.sync.dma_start(out=out_1[0].rearrange("p c r -> p (c r)").bitcast(I32), in_=y_codes[:].bitcast(I32))
+        for quad in range(4):
+            queue = nc.sync if quad % 2 else nc.scalar
+            queue.dma_start(
+                out=out_2[0, 4 * quad : 4 * quad + 4, :].bitcast(I32),
+                in_=y_scales[32 * quad : 32 * quad + 4, :].bitcast(I32),
+            )

@@ -22,7 +22,6 @@ PACK = 4
 HALVES = Q // P
 W1_SPLIT = 88
 W2_SPLIT = 352
-Y_SPLIT = 168
 
 
 def tile_attend_synthesizer_pl_kernel(tc, inp, w1, w2, size, vals, res, offs, out_0, out_1, out_2):
@@ -81,14 +80,14 @@ def tile_attend_synthesizer_pl_kernel(tc, inp, w1, w2, size, vals, res, offs, ou
         ident = sb.tile([P, P], F32)
         make_identity(nc, ident[:])
 
-        size_bank = ps.tile([P, PACK, P], F32, tag="bank4")
+        size_bank = ps.tile([P, PACK, P], F32, tag="bank7")
         for t in range(PACK):
             nc.tensor.transpose(size_bank[:, t, :], size_cols[:, t : t + 1].to_broadcast([P, P]), ident[:])
 
         size_row = sb.tile([P, I], F32)
         nc.scalar.copy(
-            out=size_row[:].rearrange("q (u g m t) -> q u g m t", u=2, m=PACK, t=PACK),
-            in_=size_bank[:].rearrange("q t (g u m) -> q u g m t", u=2, m=PACK),
+            out=size_row[:].rearrange("q (u p e) -> q u p e", u=2, e=2),
+            in_=size_bank[:].rearrange("q (u e) p -> q u p e", u=2),
         )
 
         w1_grp = sb.tile([P, F * PACK], BF16, align_bytes=64)
@@ -132,12 +131,13 @@ def tile_attend_synthesizer_pl_kernel(tc, inp, w1, w2, size, vals, res, offs, ou
         for h in range(HALVES):
             matmul(a_banks[h][:], g_ops[h][0][:], g_ops[h][1][:], w2_codes[:], w2_scales[:])
 
-        def turn(name, rows_bf16, bank_tag):
+        def turn(name, rows_bf16, dealt, bank_tag, grp_tag):
             words = rows_bf16[:].bitcast(F32)
             bank = ps.tile([P, 2, P], F32, name=name + "_bank", tag=bank_tag)
             for u in range(2):
-                nc.tensor.transpose(bank[:, u, :], words[:, u * P : (u + 1) * P], ident[:])
-            grp = sb.tile([P, P * PACK], BF16, name=name + "_grp", align_bytes=64)
+                chosen = words[:, u * P : (u + 1) * P] if dealt else words[:, u : I // 2 : 2]
+                nc.tensor.transpose(bank[:, u, :], chosen, ident[:])
+            grp = sb.tile([P, P * PACK], BF16, name=name + "_grp", align_bytes=64, tag=grp_tag)
             nc.scalar.copy(
                 out=grp[:].bitcast(F32).rearrange("p (x u) -> p x u", u=2),
                 in_=bank[:].rearrange("p u x -> p x u"),
@@ -146,13 +146,13 @@ def tile_attend_synthesizer_pl_kernel(tc, inp, w1, w2, size, vals, res, offs, ou
 
         pick = {}
 
+        def turn_vt(t):
+            return turn("vt%d" % t, pick[t], False, "bank%d" % (t % 2), "pool0" if t == 0 else "vt_grp%d" % t)
+
         def gather(t):
             picked = sb.tile([P, I], BF16, name="picked%d" % t, align_bytes=64, tag=("hold0", "hold0", "hold2", "hold3")[t])
-            nc.vector.tensor_copy(
-                picked[:].rearrange("p (u g r) -> p g u r", u=2, r=16), pools[t][:].indirect(offsets[:])
-            )
+            nc.vector.tensor_copy(picked[:], pools[t][:].indirect(offsets[:]))
             pick[t] = picked
-            return turn("vt%d" % t, picked, "bank%d" % (t % 2))
 
         vt_ops = [operand("vt%d" % t, P) if t == 3 else (None, sb.tile([P, P], U8, name="vt%d_scales" % t, align_bytes=64)) for t in range(PACK)]
 
@@ -161,15 +161,17 @@ def tile_attend_synthesizer_pl_kernel(tc, inp, w1, w2, size, vals, res, offs, ou
 
         row_sum = sb.tile([P, HALVES], F32)
         probs = [sb.tile([P, I], F32, name="probs%d" % h, align_bytes=64, tag="hold%d" % (2 + h)) for h in range(HALVES)]
-        vt_grp0 = gather(0)
+        gather(0)
         neg_max = sb.tile([P, HALVES], F32, align_bytes=64, tag="pool0")
         for h in range(HALVES):
             nc.vector.tensor_reduce(out=neg_max[:, h : h + 1], in_=a_banks[h][:], axis=AX.X, op=ALU.max, negate=True)
             nc.scalar.activation(
-                out=probs[h][:].rearrange("q (u g r) -> q u g r", u=2, r=16),
-                in_=a_banks[h][:].rearrange("q (g u r) -> q u g r", u=2, r=16), func=ACT.Exp, bias=neg_max[:, h : h + 1], scale=1.0, accum_out=row_sum[:, h : h + 1]
+                out=probs[h][:].rearrange("q (u p e) -> q u p e", u=2, e=2),
+                in_=a_banks[h][:].rearrange("q (p u e) -> q u p e", u=2, e=2), func=ACT.Exp, bias=neg_max[:, h : h + 1], scale=1.0, accum_out=row_sum[:, h : h + 1]
             )
-        vt_grp1 = gather(1)
+        vt_grp0 = turn_vt(0)
+        gather(1)
+        vt_grp1 = turn_vt(1)
         inv_sum = sb.tile([P, HALVES], F32, align_bytes=64, tag="pool1")
         nc.vector.reciprocal(out=inv_sum[:], in_=row_sum[:])
         wt_grp = []
@@ -183,9 +185,11 @@ def tile_attend_synthesizer_pl_kernel(tc, inp, w1, w2, size, vals, res, offs, ou
                 op0=ALU.mult,
                 op1=ALU.mult,
             )
-            wt_grp.append(turn("wt%d" % h, weights, "bank%d" % (5 + h)))
-        vt_grp2 = gather(2)
-        vt_grp3 = gather(3)
+            wt_grp.append(turn("wt%d" % h, weights, True, "bank%d" % (5 + h), "wt_grp%d" % h))
+        gather(2)
+        vt_grp2 = turn_vt(2)
+        gather(3)
+        vt_grp3 = turn_vt(3)
         late_codes = sb.tile([P, Q + 3 * P], U32, align_bytes=64, tag="pool3")
         wt_codes = late_codes[:, :Q]
         wt_scales = sb.tile([P, Q], U8, align_bytes=64)
@@ -201,7 +205,7 @@ def tile_attend_synthesizer_pl_kernel(tc, inp, w1, w2, size, vals, res, offs, ou
 
         o01 = ps.tile([P, 2, Q], F32, tag="bank2")
         o2 = ps.tile([P, Q], F32, tag="bank3")
-        o3 = ps.tile([P, Q], F32, tag="bank7")
+        o3 = [ps.tile([P, P], F32, name="o3_%d" % h, tag="bank%d" % (4 + 3 * h)) for h in range(HALVES)]
         y = sb.tile([P, PACK, Q], F32)
         out_rows = out_0.rearrange("(p t) q -> p t q", t=PACK)
         for t, o in ((0, o01[:, 0, :]), (1, o01[:, 1, :]), (2, o2[:])):
@@ -209,15 +213,19 @@ def tile_attend_synthesizer_pl_kernel(tc, inp, w1, w2, size, vals, res, offs, ou
         nc.vector.tensor_tensor(out=y[:, 0:2, :], in0=o01[:], in1=res_sb[:, 0:2, :], op=ALU.add)
         nc.vector.tensor_tensor(out=y[:, 2, :], in0=o2[:], in1=res_sb[:, 2, :], op=ALU.add)
         nc.sync.dma_start(out=out_rows[:, 0:3, :], in_=y[:, 0:3, :])
-        matmul(o3[:], vt_ops[3][0][:], vt_ops[3][1][:], wt_codes[:], wt_scales[:])
-        nc.vector.tensor_tensor(out=y[:, 3, :], in0=o3[:], in1=res_sb[:, 3, :], op=ALU.add)
+        halves = [slice(h * P, (h + 1) * P) for h in range(HALVES)]
+        for h in range(HALVES):
+            matmul(o3[h][:], vt_ops[3][0][:], vt_ops[3][1][:], wt_codes[:, halves[h]], wt_scales[:, halves[h]])
+        for h in range(HALVES):
+            nc.vector.tensor_tensor(out=y[:, 3, halves[h]], in0=o3[h][:], in1=res_sb[:, 3, halves[h]], op=ALU.add)
         nc.sync.dma_start(out=out_rows[:, 3, :], in_=y[:, 3, :])
 
         y_grp = sb.tile([P, Q * PACK], BF16, align_bytes=64)
-        interleave(True, y_grp, y, 0, Y_SPLIT)
-        interleave(False, y_grp, y, Y_SPLIT, Q)
         y_codes, y_scales = operand("y", Q)
-        quantize(y_codes[:], y_scales[:], y_grp[:])
+        for h in range(HALVES):
+            interleave(h == 0, y_grp, y, h * P, (h + 1) * P)
+        for h in range(HALVES):
+            quantize(y_codes[:, halves[h]], y_scales[:, halves[h]], y_grp[:, h * P * PACK : (h + 1) * P * PACK])
         nc.sync.dma_start(out=out_1[0].rearrange("p c r -> p (c r)").bitcast(I32), in_=y_codes[:].bitcast(I32))
         for quad in range(4):
             queue = nc.sync if quad % 2 else nc.scalar

from contextlib import ExitStack

import concourse.mybir as mybir
from concourse.masks import make_identity

T, I, Q, E, K, F = 2048, 512, 256, 512, 512, 512
FLOPS = 2 * Q * (K * F + F * I + I * E)

F32 = mybir.dt.float32
BF16 = mybir.dt.bfloat16
I32 = mybir.dt.int32
U32 = mybir.dt.uint32
U16 = mybir.dt.uint16
U8 = mybir.dt.uint8
FP8X4 = mybir.dt.float8_e4m3fn_x4
ALU = mybir.AluOpType
ACT = mybir.ActivationFunctionType
AX = mybir.AxisListType

P = 128
PACK = 4
HALVES = Q // P
W1_SPLIT = 88
W2_SPLIT = 352


def tile_attend_synthesizer_pl_kernel(tc, inp, w1, w2, size, vals, res, offs, out_0, out_1, out_2):
    nc = tc.nc

    with ExitStack() as ctx:
        sb = ctx.enter_context(tc.tile_pool(name="sb", bufs=1))
        ps = ctx.enter_context(tc.psum_pool(name="ps", bufs=1))

        def quantize(codes, scales, grouped):
            nc.vector.quantize_mx(out=codes.bitcast(FP8X4), scales=scales, in_=grouped)

        def matmul(out, lhs_codes, lhs_scales, rhs_codes, rhs_scales):
            nc.tensor.matmul_mx(
                out=out,
                lhsT=lhs_codes.bitcast(FP8X4),
                lhsT_scale=lhs_scales,
                rhs=rhs_codes.bitcast(FP8X4),
                rhs_scale=rhs_scales,
                start=True,
                stop=True,
            )

        def operand(name, width):
            codes = sb.tile([P, width], U32, name=name + "_codes", align_bytes=64)
            scales = sb.tile([P, width], U8, name=name + "_scales", align_bytes=64)
            return codes, scales

        def interleave(on_vector, grouped, raw, c0, c1):
            dst = grouped[:].rearrange("p (c i t) -> p c t i", i=PACK, t=PACK)[:, c0 // PACK : c1 // PACK]
            src = raw[:].rearrange("p t (c i) -> p c t i", i=PACK)[:, c0 // PACK : c1 // PACK]
            if on_vector:
                nc.vector.tensor_copy(out=dst, in_=src)
            else:
                nc.scalar.activation(out=dst, in_=src, func=ACT.Copy)

        size_cols = sb.tile([P, PACK], F32)
        nc.scalar.dma_start(out=size_cols[:], in_=size.rearrange("o (p t) -> p (o t)", t=PACK))
        w1_raw = sb.tile([P, PACK, F], F32)
        nc.sync.dma_start(out=w1_raw[:], in_=w1.rearrange("(p j) f -> p j f", j=PACK))
        inp_raw = sb.tile([P, PACK, Q], F32)
        nc.sync.dma_start(out=inp_raw[:], in_=inp.rearrange("(p j) q -> p j q", j=PACK))
        w2_raw = sb.tile([P, PACK, I], F32)
        nc.sync.dma_start(out=w2_raw[:], in_=w2.rearrange("(p j) i -> p j i", j=PACK))
        offsets = sb.tile([P, I // 16], U16)
        nc.sync.dma_start(offsets[:], offs)
        vals_rows = vals.rearrange("(p t) c -> p t c", t=PACK)
        pools = []
        for t in range(PACK):
            pool_t = sb.tile([P, T], F32, name="pool%d" % t, tag="pool%d" % t, align_bytes=64)
            nc.sync.dma_start(out=pool_t[:], in_=vals_rows[:, t, :])
            pools.append(pool_t)
        res_sb = sb.tile([P, PACK, Q], F32)
        nc.sync.dma_start(out=res_sb[:], in_=res.rearrange("(p t) q -> p t q", t=PACK))

        ident = sb.tile([P, P], F32)
        make_identity(nc, ident[:])

        size_bank = ps.tile([P, PACK, P], F32, tag="bank7")
        for t in range(PACK):
            nc.tensor.transpose(size_bank[:, t, :], size_cols[:, t : t + 1].to_broadcast([P, P]), ident[:])

        size_row = sb.tile([P, I], F32)
        nc.scalar.copy(
            out=size_row[:].rearrange("q (u p e) -> q u p e", u=2, e=2),
            in_=size_bank[:].rearrange("q (u e) p -> q u p e", u=2),
        )

        w1_grp = sb.tile([P, F * PACK], BF16, align_bytes=64)
        w1_dst = w1_grp[:].rearrange("p (t m j) -> p m j t", t=PACK, j=PACK)
        w1_src = w1_raw[:].rearrange("p j (m t) -> p m j t", t=PACK)
        nc.vector.tensor_copy(out=w1_dst[:, :W1_SPLIT], in_=w1_src[:, :W1_SPLIT])
        nc.scalar.activation(out=w1_dst[:, W1_SPLIT:], in_=w1_src[:, W1_SPLIT:], func=ACT.Copy)
        w1_codes, w1_scales = operand("w1", F)
        quantize(w1_codes[:], w1_scales[:], w1_grp[:])

        inp_grp = sb.tile([P, Q * PACK], BF16, align_bytes=64)
        interleave(True, inp_grp, inp_raw, 0, P)
        interleave(False, inp_grp, inp_raw, P, Q)
        inp_ops = [operand("inp%d" % h, P) for h in range(HALVES)]
        z_banks = [ps.tile([P, PACK, P], F32, name="z%d" % h, tag="bank%d" % h) for h in range(HALVES)]
        g_grp = [sb.tile([P, P * PACK], BF16, name="g_grp%d" % h, align_bytes=64) for h in range(HALVES)]
        for h in range(HALVES):
            quantize(inp_ops[h][0][:], inp_ops[h][1][:], inp_grp[:, h * P * PACK : (h + 1) * P * PACK])
            for t in range(PACK):
                m_cols = slice(t * P, (t + 1) * P)
                matmul(z_banks[h][:, t, :], w1_codes[:, m_cols], w1_scales[:, m_cols], inp_ops[h][0][:], inp_ops[h][1][:])

        def relu(h):
            nc.scalar.activation(
                out=g_grp[h][:].rearrange("p (q t) -> p q t", t=PACK),
                in_=z_banks[h][:].rearrange("p t q -> p q t"),
                func=ACT.Relu,
            )

        w2_grp = sb.tile([P, I * PACK], BF16, align_bytes=64, tag="hold0")
        relu(0)
        interleave(True, w2_grp, w2_raw, 0, W2_SPLIT)
        interleave(False, w2_grp, w2_raw, W2_SPLIT, I)
        relu(1)
        w2_codes, w2_scales = operand("w2", I)
        g_ops = [operand("g%d" % h, P) for h in range(HALVES)]
        quantize(g_ops[0][0][:], g_ops[0][1][:], g_grp[0][:])
        quantize(w2_codes[:], w2_scales[:], w2_grp[:])
        quantize(g_ops[1][0][:], g_ops[1][1][:], g_grp[1][:])
        a_banks = [ps.tile([P, I], F32, name="a%d" % h, tag="bank%d" % (2 + h)) for h in range(HALVES)]
        for h in range(HALVES):
            matmul(a_banks[h][:], g_ops[h][0][:], g_ops[h][1][:], w2_codes[:], w2_scales[:])

        def turn(name, rows_bf16, dealt, bank_tag, grp_tag):
            words = rows_bf16[:].bitcast(F32)
            bank = ps.tile([P, 2, P], F32, name=name + "_bank", tag=bank_tag)
            for u in range(2):
                chosen = words[:, u * P : (u + 1) * P] if dealt else words[:, u : I // 2 : 2]
                nc.tensor.transpose(bank[:, u, :], chosen, ident[:])
            grp = sb.tile([P, P * PACK], BF16, name=name + "_grp", align_bytes=64, tag=grp_tag)
            nc.scalar.copy(
                out=grp[:].bitcast(F32).rearrange("p (x u) -> p x u", u=2),
                in_=bank[:].rearrange("p u x -> p x u"),
            )
            return grp

        pick = {}

        def turn_vt(t):
            return turn("vt%d" % t, pick[t], False, "bank%d" % (t % 2), "pool0" if t == 0 else "vt_grp%d" % t)

        def gather(t):
            picked = sb.tile([P, I], BF16, name="picked%d" % t, align_bytes=64, tag=("hold0", "hold0", "hold2", "hold3")[t])
            nc.vector.tensor_copy(picked[:], pools[t][:].indirect(offsets[:]))
            pick[t] = picked

        vt_ops = [operand("vt%d" % t, P) if t == 3 else (None, sb.tile([P, P], U8, name="vt%d_scales" % t, align_bytes=64)) for t in range(PACK)]

        def quantize_vt(t, grp):
            quantize(vt_ops[t][0][:], vt_ops[t][1][:], grp[:])

        row_sum = sb.tile([P, HALVES], F32)
        probs = [sb.tile([P, I], F32, name="probs%d" % h, align_bytes=64, tag="hold%d" % (2 + h)) for h in range(HALVES)]
        gather(0)
        neg_max = sb.tile([P, HALVES], F32, align_bytes=64, tag="pool0")
        for h in range(HALVES):
            nc.vector.tensor_reduce(out=neg_max[:, h : h + 1], in_=a_banks[h][:], axis=AX.X, op=ALU.max, negate=True)
            nc.scalar.activation(
                out=probs[h][:].rearrange("q (u p e) -> q u p e", u=2, e=2),
                in_=a_banks[h][:].rearrange("q (p u e) -> q u p e", u=2, e=2), func=ACT.Exp, bias=neg_max[:, h : h + 1], scale=1.0, accum_out=row_sum[:, h : h + 1]
            )
        vt_grp0 = turn_vt(0)
        gather(1)
        vt_grp1 = turn_vt(1)
        inv_sum = sb.tile([P, HALVES], F32, align_bytes=64, tag="pool1")
        nc.vector.reciprocal(out=inv_sum[:], in_=row_sum[:])
        wt_grp = []
        for h in range(HALVES):
            weights = sb.tile([P, I], BF16, name="weights%d" % h, align_bytes=64)
            nc.vector.scalar_tensor_tensor(
                out=weights[:],
                in0=probs[h][:],
                scalar=inv_sum[:, h : h + 1],
                in1=size_row[:],
                op0=ALU.mult,
                op1=ALU.mult,
            )
            wt_grp.append(turn("wt%d" % h, weights, True, "bank%d" % (5 + h), "wt_grp%d" % h))
        gather(2)
        vt_grp2 = turn_vt(2)
        gather(3)
        vt_grp3 = turn_vt(3)
        late_codes = sb.tile([P, Q + 3 * P], U32, align_bytes=64, tag="pool3")
        wt_codes = late_codes[:, :Q]
        wt_scales = sb.tile([P, Q], U8, align_bytes=64)
        for t in range(3):
            vt_ops[t] = (late_codes[:, Q + t * P : Q + (t + 1) * P], vt_ops[t][1])
        for h in range(HALVES):
            q_cols = slice(h * P, (h + 1) * P)
            quantize(wt_codes[:, q_cols], wt_scales[:, q_cols], wt_grp[h][:])
        quantize_vt(0, vt_grp0)
        quantize_vt(1, vt_grp1)
        quantize_vt(2, vt_grp2)
        quantize_vt(3, vt_grp3)

        o01 = ps.tile([P, 2, Q], F32, tag="bank2")
        o2 = ps.tile([P, Q], F32, tag="bank3")
        o3 = [ps.tile([P, P], F32, name="o3_%d" % h, tag="bank%d" % (4 + 3 * h)) for h in range(HALVES)]
        y = sb.tile([P, PACK, Q], F32)
        out_rows = out_0.rearrange("(p t) q -> p t q", t=PACK)
        for t, o in ((0, o01[:, 0, :]), (1, o01[:, 1, :]), (2, o2[:])):
            matmul(o, vt_ops[t][0][:], vt_ops[t][1][:], wt_codes[:], wt_scales[:])
        nc.vector.tensor_tensor(out=y[:, 0:2, :], in0=o01[:], in1=res_sb[:, 0:2, :], op=ALU.add)
        nc.vector.tensor_tensor(out=y[:, 2, :], in0=o2[:], in1=res_sb[:, 2, :], op=ALU.add)
        nc.sync.dma_start(out=out_rows[:, 0:3, :], in_=y[:, 0:3, :])
        halves = [slice(h * P, (h + 1) * P) for h in range(HALVES)]
        for h in range(HALVES):
            matmul(o3[h][:], vt_ops[3][0][:], vt_ops[3][1][:], wt_codes[:, halves[h]], wt_scales[:, halves[h]])
        for h in range(HALVES):
            nc.vector.tensor_tensor(out=y[:, 3, halves[h]], in0=o3[h][:], in1=res_sb[:, 3, halves[h]], op=ALU.add)
        nc.sync.dma_start(out=out_rows[:, 3, :], in_=y[:, 3, :])

        y_grp = sb.tile([P, Q * PACK], BF16, align_bytes=64)
        y_codes, y_scales = operand("y", Q)
        for h in range(HALVES):
            interleave(h == 0, y_grp, y, h * P, (h + 1) * P)
        for h in range(HALVES):
            quantize(y_codes[:, halves[h]], y_scales[:, halves[h]], y_grp[:, h * P * PACK : (h + 1) * P * PACK])
        nc.sync.dma_start(out=out_1[0].rearrange("p c r -> p (c r)").bitcast(I32), in_=y_codes[:].bitcast(I32))
        for quad in range(4):
            queue = nc.sync if quad % 2 else nc.scalar
            queue.dma_start(
                out=out_2[0, 4 * quad : 4 * quad + 4, :].bitcast(I32),
                in_=y_scales[32 * quad : 32 * quad + 4, :].bitcast(I32),
            )
